import numpy as np
import ml_dtypes


def mxq(x, axis, fmt="e4m3"):
    dtype, down = {"e4m3": (ml_dtypes.float8_e4m3fn, 7), "e5m2": (ml_dtypes.float8_e5m2, 14)}[fmt]
    v = np.moveaxis(np.asarray(x, np.float32).astype(ml_dtypes.bfloat16).astype(np.float64), axis, -1)
    blocks = v.reshape(v.shape[:-1] + (-1, 32))
    amax = np.abs(blocks).max(-1, keepdims=True)
    byte = np.maximum(np.where(amax > 0, np.frexp(amax)[1] - 1 + 127, 0) - down, 1)
    scale = np.exp2(byte - 127.0)
    codes = (blocks / scale).astype(np.float32).astype(dtype).astype(np.float64)
    return np.moveaxis((codes * scale).reshape(v.shape), -1, axis)


WIDE = False


def mx_kscale(k):
    if not WIDE:
        return np.ones(k)
    levels = np.array([10, -10, 5, -5, 0])
    if k % 512:
        return np.exp2(np.random.permutation(np.resize(levels, k // 32))).repeat(32)
    a = np.empty((k // 512, 16))
    for p in range(k // 512):
        a[p, :8] = np.random.permutation(np.resize(levels, 8))
        for g in range(8):
            far = levels[np.abs(levels - a[p, g]) >= 10]
            a[p, g + 8] = far[np.random.randint(len(far))]
    return np.exp2(a.ravel()).repeat(32)


def f64(x):
    return np.asarray(x).astype(np.float64)


def striped(idx):
    return np.tile(idx.reshape(-1, 16).T, (8, 1)).astype(np.uint16)


def unstriped(offs):
    return offs[:16].T.reshape(-1).astype(np.int64)


E2M1 = np.array([0.0, 0.5, 1.0, 1.5, 2.0, 3.0, 4.0, 6.0, -0.0, -0.5, -1.0, -1.5, -2.0, -3.0, -4.0, -6.0])


def pack_weight(w, fmt):
    k, n = w.shape
    w = f64(np.asarray(w, np.float32).astype(ml_dtypes.bfloat16)).reshape(k // 32, 32, n)
    amax = np.abs(w).max(1)
    if fmt == "e4m3":
        byte = np.frexp(amax)[1] - 1 + 127 - 7
    else:
        mant, ex = np.frexp(amax / 6.0)
        byte = np.where(mant > 0.5, ex, ex - 1) + 127
    byte = np.clip(np.where(amax > 0, byte, 1), 1, 254)
    scaled = (w * np.exp2(127.0 - byte)[:, None, :]).reshape(k, n).astype(np.float32)
    by_word = np.ascontiguousarray(scaled.reshape(k // 512, 128, 4, n).transpose(0, 1, 3, 2))
    if fmt == "e4m3":
        words = by_word.astype(ml_dtypes.float8_e4m3fn).view(np.uint8)
    else:
        c = by_word.astype(ml_dtypes.float4_e2m1fn).view(np.uint8) & 0xF
        words = (c[..., 0::2] | (c[..., 1::2] << 4)).reshape(k // 512, 128, 2 * n)
    return np.ascontiguousarray(words), np.ascontiguousarray(byte.astype(np.uint8).reshape(k // 512, 16, n))


def unpack_weight(words, scales, fmt):
    g, _, n = scales.shape
    words = np.ascontiguousarray(words).reshape(g, 128, n, -1)
    if fmt == "e4m3":
        vals = words.view(ml_dtypes.float8_e4m3fn).astype(np.float64)
    else:
        nib = np.empty((g, 128, n, 4), np.uint8)
        nib[..., 0::2] = words & 0xF
        nib[..., 1::2] = words >> 4
        vals = E2M1[nib]
    vals = vals * np.repeat(np.exp2(scales.astype(np.float64) - 127.0), 8, axis=1)[..., None]
    return vals.transpose(0, 1, 3, 2).reshape(g * 512, n)


def relu(v):
    return np.maximum(v, 0.0)


K, T, E, C, H, N = 1024, 640, 15, 128, 512, 128
TOP = 3


def by_expert(wq, xq):
    return np.concatenate([wq[e].T @ xq[:, e * C:(e + 1) * C] for e in range(E)], axis=1)


def setup_inputs():
    n = np.random.standard_normal
    s = mx_kscale(K)[:, None]
    u = mx_kscale(H)
    deal = np.repeat(np.arange(E), C).reshape(TOP, T)[:, np.random.permutation(T)]
    deal = np.take_along_axis(deal, np.argsort(np.random.rand(TOP, T), axis=0), axis=0)
    for _ in range(8):
        s_, t_ = np.random.permutation(T).reshape(2, -1); r = np.random.randint(TOP, size=T // 2); x, y = deal[r, s_].copy(), deal[r, t_].copy()
        ok = ~((deal[:, s_] == y).any(0) | (deal[:, t_] == x).any(0)); deal[r[ok], s_[ok]] = y[ok]; deal[r[ok], t_[ok]] = x[ok]
    order = np.lexsort((np.random.rand(TOP * T), deal.reshape(-1)))
    slot_token = order % T; pos = np.empty(TOP * T, np.int64); pos[order] = np.arange(TOP * T); pos = pos.reshape(TOP, T)
    g = np.random.uniform(0.5, 1.5, (TOP, T)); g = g / g.sum(0)
    w1 = [pack_weight(m, "e2m1") for m in n((E, K, H)) / np.sqrt(K) / s[None] * u[None, None, :]]
    w2 = [pack_weight(m, "e2m1") for m in n((E, H, N)) / np.sqrt(H) / u[None, :, None]]
    return {
        "xT": (n((K, T)) * s).astype(np.float32),
        "w1_words": np.stack([m[0] for m in w1]),
        "w1_scales": np.stack([m[1] for m in w1]),
        "w2_words": np.stack([m[0] for m in w2]),
        "w2_scales": np.stack([m[1] for m in w2]),
        "gate": np.stack([np.tile(r, (N, 1)) for r in g]).astype(np.float32),
        "offs": striped(slot_token),
        "pos1": striped(pos[0]),
        "pos2": striped(pos[1]),
        "pos3": striped(pos[2]),
    }


def reference(xT, w1_words, w1_scales, w2_words, w2_scales, gate, offs, pos1, pos2, pos3):
    idx = unstriped(offs)
    w1 = np.stack([unpack_weight(w1_words[e], w1_scales[e], "e2m1") for e in range(E)])
    w2 = np.stack([unpack_weight(w2_words[e], w2_scales[e], "e2m1") for e in range(E)])
    xq = mxq(f64(xT)[:, idx], 0, "e4m3")
    h = relu(by_expert(w1, xq))
    y = by_expert(w2, mxq(h, 0, "e4m3"))
    return sum(f64(gate[r]) * y[:, unstriped(p)] for r, p in enumerate((pos1, pos2, pos3)))

@@ -1,0 +1,246 @@
+from contextlib import ExitStack
+
+import concourse.mybir as mybir
+from concourse.masks import make_identity
+
+F32 = mybir.dt.float32
+BF16 = mybir.dt.bfloat16
+I32 = mybir.dt.int32
+U32 = mybir.dt.uint32
+U16 = mybir.dt.uint16
+U8 = mybir.dt.uint8
+FP8X4 = mybir.dt.float8_e4m3fn_x4
+FP4X4 = mybir.dt.float4_e2m1fn_x4
+ACT = mybir.ActivationFunctionType
+MULT = mybir.AluOpType.mult
+ADD = mybir.AluOpType.add
+
+P = 128
+K, T, E, C, H, N = 1024, 640, 15, 128, 512, 128
+TOP = 3
+S = E * C
+PASSES = K // 512
+FLOPS = 2 * S * H * (K + N)
+
+CHUNKS = ((0, 1), (1, 3), (3, 6), (6, 9), (9, 12), (12, 15))
+W_LOADS = ((0, 2), (2, 5), (5, 8), (8, 11), (11, 15))
+SHIFTS = {0: (0, 1), 2: (1, 6), 3: (6, 9), 5: (9, 15)}
+BATCHES = ((0, 4), (4, 8), (8, 12), (12, 14), (14, 15))
+VECTOR_TURNS = (10, 12, 14)
+OUT_PARTS = ((0, 512), (512, 640))
+T_LOADS = ((0, 640),)
+T_PARTS = ((0, 256), (256, 512), (512, 640))
+
+
+def tile_moe_tk_mlp_relu_kernel(tc, xT, w1_words, w1_scales, w2_words, w2_scales, gate, offs, pos1, pos2, pos3, out):
+    nc = tc.nc
+    with ExitStack() as ctx:
+        lists = ctx.enter_context(tc.tile_pool(name="lists", bufs=1))
+        keep = ctx.enter_context(tc.tile_pool(name="keep", bufs=1))
+        gring = ctx.enter_context(tc.tile_pool(name="gring", bufs=4))
+        ring = ctx.enter_context(tc.tile_pool(name="ring", bufs=4))
+        psum_a = ctx.enter_context(tc.psum_pool(name="psum_a", bufs=5))
+        psum_t = ctx.enter_context(tc.psum_pool(name="psum_t", bufs=2))
+        psum_y = ctx.enter_context(tc.psum_pool(name="psum_y", bufs=1))
+
+        offs_t = lists.tile([P, S // 16], U16, name="offs_t")
+        pos_t = [lists.tile([P, T // 16], U16, name="pos_t%d" % r) for r in range(TOP)]
+
+        w1s = keep.tile([P, E * PASSES * H], U8, align_bytes=64, name="w1s")
+        w2s = keep.tile([P, E * N], U8, align_bytes=64, name="w2s")
+        xs = keep.tile([P, T], U8, align_bytes=64, name="xs")
+        gs1 = keep.tile([P, S], U8, align_bytes=64, name="gs1")
+        for t in (w2s, w1s, xs, gs1):
+            nc.vector.memset(t[:].bitcast(I32), 0)
+
+        w1s_view = w1_scales.rearrange("e s q i -> q (e s) i").bitcast(I32)
+        w2s_view = w2_scales.rearrange("e s q n -> q (e s) n").bitcast(I32)
+        for q in range(4):
+            nc.gpsimd.dma_start(
+                out=w2s[32 * q : 32 * q + 4, :].bitcast(I32).rearrange("q (a n) -> q a n", n=N // 4),
+                in_=w2s_view[4 * q : 4 * q + 4, :, :],
+            )
+        ident = keep.tile([P, P], F32, name="ident")
+        make_identity(nc, ident[:])
+
+        x_view = xT.rearrange("(s p j) t -> s p j t", p=P, j=4)
+        x_raw = {}
+        for s in range(PASSES):
+            for a, b in T_LOADS:
+                raw = keep.tile([P, 4, b - a], F32, name="x_raw_%d_%d" % (s, a))
+                nc.sync.dma_start(out=raw[:], in_=x_view[s, :, :, a:b])
+                x_raw[s, a] = raw
+            if s == 0:
+                nc.sync.dma_start(offs_t[:], offs)
+                for r, pos in enumerate((pos1, pos2, pos3)):
+                    nc.sync.dma_start(pos_t[r][:], pos)
+
+        w1 = {}
+        w1_view = w1_words.rearrange("e s p b -> p e s b").bitcast(I32)
+
+        def load_w1(a, b):
+            w = keep.tile([P, b - a, PASSES, 2 * H], U8, align_bytes=64, name="w1_%d" % a)
+            nc.sync.dma_start(out=w[:].bitcast(I32), in_=w1_view[:, a:b])
+            for e in range(a, b):
+                w1[e] = (w, e - a)
+
+        load_w1(*W_LOADS[0])
+        for q in range(4):
+            nc.sync.dma_start(
+                out=w1s[32 * q : 32 * q + 4, :].bitcast(I32).rearrange("q (a i) -> q a i", i=H // 4),
+                in_=w1s_view[4 * q : 4 * q + 4, :, :],
+            )
+
+        def load_rest():
+            nc.sync.dma_start(out=w2[:].bitcast(I32), in_=w2_words.rearrange("e s p b -> p (e s) b").bitcast(I32))
+
+        w2 = keep.tile([P, E, 2 * N], U8, align_bytes=64, name="w2")
+
+        xw = [keep.tile([P, T], U32, align_bytes=64, name="xw%d" % s) for s in range(PASSES)]
+        gw = {}
+        gs = keep.tile([P, S], U8, align_bytes=64, name="gs")
+
+        def interleave(s, i, engine):
+            a, b = T_PARTS[i]
+            load = max(l[0] for l in T_LOADS if l[0] <= a)
+            raw = x_raw[s, load]
+            xb = keep.tile([P, b - a, 4], BF16, align_bytes=64, name="xb_%d_%d" % (s, a))
+            src = raw[:, :, a - load : b - load].rearrange("p j t -> p t j")
+            if engine == "v":
+                nc.vector.tensor_copy(out=xb[:], in_=src)
+            else:
+                nc.scalar.copy(out=xb[:], in_=src)
+            return xb
+
+        def quantise_x(s, i, xb):
+            a, b = T_PARTS[i]
+            nc.vector.quantize_mx(
+                out=xw[s][:, a:b].bitcast(FP8X4),
+                scales=xs[4 * s : P, a:b],
+                in_=xb[:].rearrange("p t j -> p (t j)"),
+            )
+
+        def gather_words(s, c):
+            a, b = CHUNKS[c][0] * C, CHUNKS[c][1] * C
+            if s == 0:
+                words = gring.tile([P, 3 * C], U32, align_bytes=64, name="words")
+            else:
+                words = keep.tile([P, b - a], U32, align_bytes=64, name="words1_%d" % c)
+            nc.vector.tensor_copy(out=words[:, : b - a], in_=xw[s][:].indirect(offs_t[:, a // 16 : b // 16]))
+            for e in range(*CHUNKS[c]):
+                gw[s, e] = words[:, e * C - a : (e + 1) * C - a]
+
+        def gather_scales(c):
+            a, b = CHUNKS[c][0] * C, CHUNKS[c][1] * C
+            nc.vector.tensor_copy(out=gs[:, a:b], in_=xs[:].indirect(offs_t[:, a // 16 : b // 16]))
+            if CHUNKS[c][1] in [x[1] for x in SHIFTS.values()]:
+                lo = [x for x in SHIFTS.values() if x[1] == CHUNKS[c][1]][0][0] * C
+                nc.scalar.dma_start(out=gs1[0:112, lo:b].bitcast(I32), in_=gs[4:116, lo:b].bitcast(I32))
+
+        load_rest()
+        for a, b in W_LOADS[1:]:
+            load_w1(a, b)
+        gates = keep.tile([P, TOP, T], F32, name="gates")
+        nc.sync.dma_start(out=gates[:], in_=gate.rearrange("r n t -> n r t"))
+
+        for s, engines in ((0, "svv"), (1, "svv")):
+            xbs = [interleave(s, i, engines[i]) for i in range(3)]
+            for i in range(3):
+                quantise_x(s, i, xbs[i])
+            if s == 0:
+                gather_words(0, 0)
+                gather_words(0, 1)
+        gather_scales(0)
+        gather_words(1, 0)
+        gather_scales(1)
+        gather_scales(2)
+        gather_words(1, 1)
+        gather_words(0, 2)
+        gather_words(1, 2)
+        gather_words(0, 3)
+        gather_scales(3)
+        gather_words(1, 3)
+        gather_scales(4)
+        gather_scales(5)
+
+        y_all = keep.tile([P, S], F32, name="y_all")
+
+        def first_layer(e):
+            acc = psum_a.tile([C, H], F32, name="acc")
+            w, at = w1[e]
+            slots = slice(e * C, (e + 1) * C)
+            for s in range(PASSES):
+                cols = slice((e * PASSES + s) * H, (e * PASSES + s + 1) * H)
+                nc.tensor.matmul_mx(
+                    out=acc[:],
+                    lhsT=gw[s, e].bitcast(FP8X4),
+                    lhsT_scale=(gs, gs1)[s][:, slots],
+                    rhs=w[:, at, s, :].bitcast(FP4X4),
+                    rhs_scale=w1s[:, cols],
+                    start=(s == 0),
+                    stop=(s == PASSES - 1),
+                )
+            h = ring.tile([C, 2, P, 2], BF16, name="h")
+            nc.scalar.activation(out=h[:], in_=acc[:].rearrange("c (p u d) -> c u p d", u=2, d=2), func=ACT.Relu)
+            return h[:].rearrange("c u p d -> c (u p d)").bitcast(F32)
+
+        def turn(a, b, hb):
+            n = b - a
+            ht = psum_t.tile([P, n, 2, C], F32, name="ht")
+            for e in range(a, b):
+                pairs = first_layer(e)
+                for u in range(2):
+                    nc.tensor.transpose(ht[:, e - a, u, :], pairs[:, u * P : (u + 1) * P], ident[:])
+            copy = nc.vector.tensor_copy if a in VECTOR_TURNS else nc.scalar.copy
+            copy(
+                out=hb.rearrange("p c d -> p (c d)").bitcast(F32).rearrange("p (g c u) -> p g c u", g=n, u=2),
+                in_=ht[:].rearrange("p g u c -> p g c u"),
+            )
+
+        def second_layer(a, b, hb):
+            n = b - a
+            hw = keep.tile([P, n * C], U32, align_bytes=64, name="hw_%d" % a)
+            hs = keep.tile([P, n * C], U8, align_bytes=64, name="hs_%d" % a)
+            nc.vector.quantize_mx(out=hw[:].bitcast(FP8X4), scales=hs[:], in_=hb[:].rearrange("p c d -> p (c d)"))
+            y = psum_y.tile([N, n * C], F32, name="y")
+            for e in range(a, b):
+                cols = slice((e - a) * C, (e - a + 1) * C)
+                nc.tensor.matmul_mx(
+                    out=y[:, cols],
+                    lhsT=w2[:, e, :].bitcast(FP4X4),
+                    lhsT_scale=w2s[:, e * N : (e + 1) * N],
+                    rhs=hw[:, cols].bitcast(FP8X4),
+                    rhs_scale=hs[:, cols],
+                    start=True,
+                    stop=True,
+                )
+            nc.scalar.copy(out=y_all[:, a * C : b * C], in_=y[:])
+
+        gathered = 4
+        for i, (a, b) in enumerate(BATCHES):
+            hb = keep.tile([P, (b - a) * C, 4], BF16, align_bytes=64, name="hb_%d" % a)
+            for e in range(a, b, 2):
+                f = min(e + 2, b)
+                while gathered < len(CHUNKS) and CHUNKS[gathered - 4][1] <= e:
+                    gather_words(0, gathered)
+                    gather_words(1, gathered)
+                    gathered += 1
+                turn(e, f, hb[:, (e - a) * C : (f - a) * C, :])
+            second_layer(a, b, hb)
+
+        for a, b in OUT_PARTS:
+            prods = []
+            for r in range(TOP):
+                prod = keep.tile([N, b - a], F32, name="prod_%d_%d" % (a, r))
+                nc.vector.tensor_tensor(
+                    out=prod[:],
+                    in0=y_all[:].indirect(pos_t[r][:, a // 16 : b // 16]),
+                    in1=gates[:, r, a:b],
+                    op=MULT,
+                )
+                prods.append(prod)
+            part = keep.tile([N, b - a], F32, name="part_%d" % a)
+            nc.vector.tensor_tensor(out=part[:], in0=prods[0][:], in1=prods[1][:], op=ADD)
+            result = keep.tile([N, b - a], F32, name="result_%d" % a)
+            nc.vector.tensor_tensor(out=result[:], in0=part[:], in1=prods[2][:], op=ADD)
+            nc.sync.dma_start(out=out[:, a:b], in_=result[:])

@@ -22,14 +22,14 @@ S = E * C
 PASSES = K // 512
 FLOPS = 2 * S * H * (K + N)
 
-CHUNKS = ((0, 1), (1, 3), (3, 6), (6, 9), (9, 12), (12, 15))
-W_LOADS = ((0, 2), (2, 5), (5, 8), (8, 11), (11, 15))
-SHIFTS = {0: (0, 1), 2: (1, 6), 3: (6, 9), 5: (9, 15)}
+SCALE_RUNS = ((0, 3), (3, 9), (9, 15))
+W_LOADS = (((0, 1), (1, 2)), ((2, 4),), ((4, 7), (7, 9)), ((9, 12), (12, 15)))
+EARLY = 2
+CHUNKS = ((2, 4), (4, 7), (7, 10), (10, 13), (13, 15))
+X_PARTS = (((0, 256, "v"), (256, 384, "v"), (384, 640, "s")), ((0, 256, "v"), (256, 512, "s"), (512, 640, "s")))
+TURNS = ((0, 2), (2, 4), (4, 6), (6, 8), (8, 10), (10, 12), (12, 14), (14, 15))
 BATCHES = ((0, 4), (4, 8), (8, 12), (12, 14), (14, 15))
-VECTOR_TURNS = (10, 12, 14)
 OUT_PARTS = ((0, 512), (512, 640))
-T_LOADS = ((0, 640),)
-T_PARTS = ((0, 256), (256, 512), (512, 640))
 
 
 def tile_moe_tk_mlp_relu_kernel(tc, xT, w1_words, w1_scales, w2_words, w2_scales, gate, offs, pos1, pos2, pos3, out):
@@ -37,46 +37,34 @@ def tile_moe_tk_mlp_relu_kernel(tc, xT, w1_words, w1_scales, w2_words, w2_scales
     with ExitStack() as ctx:
         lists = ctx.enter_context(tc.tile_pool(name="lists", bufs=1))
         keep = ctx.enter_context(tc.tile_pool(name="keep", bufs=1))
-        gring = ctx.enter_context(tc.tile_pool(name="gring", bufs=4))
         ring = ctx.enter_context(tc.tile_pool(name="ring", bufs=4))
-        psum_a = ctx.enter_context(tc.psum_pool(name="psum_a", bufs=5))
+        psum_a = ctx.enter_context(tc.psum_pool(name="psum_a", bufs=4))
         psum_t = ctx.enter_context(tc.psum_pool(name="psum_t", bufs=2))
-        psum_y = ctx.enter_context(tc.psum_pool(name="psum_y", bufs=1))
+        psum_y = ctx.enter_context(tc.psum_pool(name="psum_y", bufs=2))
 
         offs_t = lists.tile([P, S // 16], U16, name="offs_t")
         pos_t = [lists.tile([P, T // 16], U16, name="pos_t%d" % r) for r in range(TOP)]
 
-        w1s = keep.tile([P, E * PASSES * H], U8, align_bytes=64, name="w1s")
+        w1s = [keep.tile([P, (b - a) * PASSES * H], U8, align_bytes=64, name="w1s_%d" % a) for a, b in SCALE_RUNS]
         w2s = keep.tile([P, E * N], U8, align_bytes=64, name="w2s")
-        xs = keep.tile([P, T], U8, align_bytes=64, name="xs")
-        gs1 = keep.tile([P, S], U8, align_bytes=64, name="gs1")
-        for t in (w2s, w1s, xs, gs1):
+        xs = [keep.tile([P, T], U8, align_bytes=64, name="xs%d" % s) for s in range(PASSES)]
+        for t in w1s[:1] + xs + w1s[1:] + [w2s]:
             nc.vector.memset(t[:].bitcast(I32), 0)
-
-        w1s_view = w1_scales.rearrange("e s q i -> q (e s) i").bitcast(I32)
-        w2s_view = w2_scales.rearrange("e s q n -> q (e s) n").bitcast(I32)
-        for q in range(4):
-            nc.gpsimd.dma_start(
-                out=w2s[32 * q : 32 * q + 4, :].bitcast(I32).rearrange("q (a n) -> q a n", n=N // 4),
-                in_=w2s_view[4 * q : 4 * q + 4, :, :],
-            )
         ident = keep.tile([P, P], F32, name="ident")
         make_identity(nc, ident[:])
 
         x_view = xT.rearrange("(s p j) t -> s p j t", p=P, j=4)
-        x_raw = {}
-        for s in range(PASSES):
-            for a, b in T_LOADS:
-                raw = keep.tile([P, 4, b - a], F32, name="x_raw_%d_%d" % (s, a))
-                nc.sync.dma_start(out=raw[:], in_=x_view[s, :, :, a:b])
-                x_raw[s, a] = raw
-            if s == 0:
-                nc.sync.dma_start(offs_t[:], offs)
-                for r, pos in enumerate((pos1, pos2, pos3)):
-                    nc.sync.dma_start(pos_t[r][:], pos)
+        x_raw = [keep.tile([P, 4, T], F32, align_bytes=64, name="x_raw%d" % s, tag="x_raw%d" % s) for s in range(PASSES)]
+        nc.sync.dma_start(out=x_raw[0][:], in_=x_view[0])
+        nc.sync.dma_start(offs_t[:], offs)
+        for r, pos in enumerate((pos1, pos2, pos3)):
+            nc.sync.dma_start(pos_t[r][:], pos)
+        nc.sync.dma_start(out=x_raw[1][:], in_=x_view[1])
 
         w1 = {}
         w1_view = w1_words.rearrange("e s p b -> p e s b").bitcast(I32)
+        w1s_view = w1_scales.rearrange("e s (q r) i -> r q (e s) i", r=4).bitcast(I32)
+        w2s_view = w2_scales.rearrange("e s (q r) n -> r q (e s) n", r=4).bitcast(I32)
 
         def load_w1(a, b):
             w = keep.tile([P, b - a, PASSES, 2 * H], U8, align_bytes=64, name="w1_%d" % a)
@@ -84,99 +72,87 @@ def tile_moe_tk_mlp_relu_kernel(tc, xT, w1_words, w1_scales, w2_words, w2_scales
             for e in range(a, b):
                 w1[e] = (w, e - a)
 
-        load_w1(*W_LOADS[0])
-        for q in range(4):
-            nc.sync.dma_start(
-                out=w1s[32 * q : 32 * q + 4, :].bitcast(I32).rearrange("q (a i) -> q a i", i=H // 4),
-                in_=w1s_view[4 * q : 4 * q + 4, :, :],
-            )
-
-        def load_rest():
-            nc.sync.dma_start(out=w2[:].bitcast(I32), in_=w2_words.rearrange("e s p b -> p (e s) b").bitcast(I32))
-
-        w2 = keep.tile([P, E, 2 * N], U8, align_bytes=64, name="w2")
-
-        xw = [keep.tile([P, T], U32, align_bytes=64, name="xw%d" % s) for s in range(PASSES)]
-        gw = {}
-        gs = keep.tile([P, S], U8, align_bytes=64, name="gs")
-
-        def interleave(s, i, engine):
-            a, b = T_PARTS[i]
-            load = max(l[0] for l in T_LOADS if l[0] <= a)
-            raw = x_raw[s, load]
-            xb = keep.tile([P, b - a, 4], BF16, align_bytes=64, name="xb_%d_%d" % (s, a))
-            src = raw[:, :, a - load : b - load].rearrange("p j t -> p t j")
-            if engine == "v":
-                nc.vector.tensor_copy(out=xb[:], in_=src)
-            else:
-                nc.scalar.copy(out=xb[:], in_=src)
-            return xb
-
-        def quantise_x(s, i, xb):
-            a, b = T_PARTS[i]
-            nc.vector.quantize_mx(
-                out=xw[s][:, a:b].bitcast(FP8X4),
-                scales=xs[4 * s : P, a:b],
-                in_=xb[:].rearrange("p t j -> p (t j)"),
-            )
-
-        def gather_words(s, c):
-            a, b = CHUNKS[c][0] * C, CHUNKS[c][1] * C
-            if s == 0:
-                words = gring.tile([P, 3 * C], U32, align_bytes=64, name="words")
-            else:
-                words = keep.tile([P, b - a], U32, align_bytes=64, name="words1_%d" % c)
-            nc.vector.tensor_copy(out=words[:, : b - a], in_=xw[s][:].indirect(offs_t[:, a // 16 : b // 16]))
-            for e in range(*CHUNKS[c]):
-                gw[s, e] = words[:, e * C - a : (e + 1) * C - a]
-
-        def gather_scales(c):
-            a, b = CHUNKS[c][0] * C, CHUNKS[c][1] * C
-            nc.vector.tensor_copy(out=gs[:, a:b], in_=xs[:].indirect(offs_t[:, a // 16 : b // 16]))
-            if CHUNKS[c][1] in [x[1] for x in SHIFTS.values()]:
-                lo = [x for x in SHIFTS.values() if x[1] == CHUNKS[c][1]][0][0] * C
-                nc.scalar.dma_start(out=gs1[0:112, lo:b].bitcast(I32), in_=gs[4:116, lo:b].bitcast(I32))
-
-        load_rest()
-        for a, b in W_LOADS[1:]:
+        for a, b in W_LOADS[0]:
             load_w1(a, b)
+        for g, (lo, hi) in enumerate(SCALE_RUNS):
+            for r in range(4):
+                nc.sync.dma_start(
+                    out=w1s[g][r:P:32, :].bitcast(I32).rearrange("q (a i) -> q a i", i=H // 4),
+                    in_=w1s_view[r, :, lo * PASSES : hi * PASSES, :],
+                )
+            for a, b in W_LOADS[g + 1]:
+                load_w1(a, b)
+        for r in range(4):
+            nc.sync.dma_start(
+                out=w2s[r:P:32, :].bitcast(I32).rearrange("q (a n) -> q a n", n=N // 4),
+                in_=w2s_view[r],
+            )
+        w2 = keep.tile([P, E, 2 * N], U8, align_bytes=64, name="w2")
+        nc.sync.dma_start(out=w2[:].bitcast(I32), in_=w2_words.rearrange("e s p b -> p (e s) b").bitcast(I32))
         gates = keep.tile([P, TOP, T], F32, name="gates")
         nc.sync.dma_start(out=gates[:], in_=gate.rearrange("r n t -> n r t"))
 
-        for s, engines in ((0, "svv"), (1, "svv")):
-            xbs = [interleave(s, i, engines[i]) for i in range(3)]
-            for i in range(3):
-                quantise_x(s, i, xbs[i])
-            if s == 0:
-                gather_words(0, 0)
-                gather_words(0, 1)
-        gather_scales(0)
-        gather_words(1, 0)
-        gather_scales(1)
-        gather_scales(2)
-        gather_words(1, 1)
-        gather_words(0, 2)
-        gather_words(1, 2)
-        gather_words(0, 3)
-        gather_scales(3)
-        gather_words(1, 3)
-        gather_scales(4)
-        gather_scales(5)
+        xw = [keep.tile([P, T], U32, align_bytes=64, name="xw%d" % s) for s in range(PASSES)]
+        gw = {}
+        gs = {}
+
+        def interleave(s, a, b, engine):
+            xb = keep.tile([P, b - a, 4], BF16, align_bytes=64, name="xb", tag="xb_%d_%d" % (s, a))
+            copy = nc.vector.tensor_copy if engine == "v" else nc.scalar.copy
+            copy(
+                out=xb[:].rearrange("p (c i) j -> p c j i", i=4),
+                in_=x_raw[s][:, :, a:b].rearrange("p j (c i) -> p c j i", i=4),
+            )
+            return xb
+
+        def quantise_x(s):
+            xbs = [interleave(s, a, b, engine) for a, b, engine in X_PARTS[s]]
+            for xb, (a, b, engine) in zip(xbs, X_PARTS[s]):
+                nc.vector.quantize_mx(
+                    out=xw[s][:, a:b].bitcast(FP8X4),
+                    scales=xs[s][:, a:b],
+                    in_=xb[:].rearrange("p t j -> p (t j)"),
+                )
+
+        def gather(s, a, b, words, scales):
+            picks = offs_t[:, a * C // 16 : b * C // 16]
+            nc.vector.tensor_copy(out=scales, in_=xs[s][:].indirect(picks))
+            nc.vector.tensor_copy(out=words, in_=xw[s][:].indirect(picks))
+            for e in range(a, b):
+                gw[s, e] = words[:, (e - a) * C : (e - a + 1) * C]
+                gs[s, e] = scales[:, (e - a) * C : (e - a + 1) * C]
+
+        def gather_fresh(s, a, b):
+            words = keep.tile([P, (b - a) * C], U32, align_bytes=64, name="words", tag="gw_%d_%d" % (s, a))
+            scales = keep.tile([P, (b - a) * C], U8, align_bytes=64, name="scales", tag="gs_%d_%d" % (s, a))
+            gather(s, a, b, words[:], scales[:])
+
+        quantise_x(0)
+        gather_fresh(0, 0, EARLY)
+        quantise_x(1)
+        for e in range(EARLY):
+            gather_fresh(1, e, e + 1)
+        late_w = keep.tile([P, (E - EARLY) * C], U32, align_bytes=64, name="late_w", tag="x_raw1")
+        late_s = keep.tile([P, (E - EARLY) * C], U8, align_bytes=64, name="late_s", tag="xb_1_0")
+        for a, b in CHUNKS:
+            cols = slice((a - EARLY) * C, (b - EARLY) * C)
+            gather(0, a, b, late_w[:, cols], late_s[:, cols])
+            gather_fresh(1, a, b)
 
         y_all = keep.tile([P, S], F32, name="y_all")
 
         def first_layer(e):
             acc = psum_a.tile([C, H], F32, name="acc")
             w, at = w1[e]
-            slots = slice(e * C, (e + 1) * C)
+            g = [i for i, run in enumerate(SCALE_RUNS) if run[0] <= e < run[1]][0]
             for s in range(PASSES):
-                cols = slice((e * PASSES + s) * H, (e * PASSES + s + 1) * H)
+                col = ((e - SCALE_RUNS[g][0]) * PASSES + s) * H
                 nc.tensor.matmul_mx(
                     out=acc[:],
                     lhsT=gw[s, e].bitcast(FP8X4),
-                    lhsT_scale=(gs, gs1)[s][:, slots],
+                    lhsT_scale=gs[s, e],
                     rhs=w[:, at, s, :].bitcast(FP4X4),
-                    rhs_scale=w1s[:, cols],
+                    rhs_scale=w1s[g][:, col : col + H],
                     start=(s == 0),
                     stop=(s == PASSES - 1),
                 )
@@ -184,24 +160,35 @@ def tile_moe_tk_mlp_relu_kernel(tc, xT, w1_words, w1_scales, w2_words, w2_scales
             nc.scalar.activation(out=h[:], in_=acc[:].rearrange("c (p u d) -> c u p d", u=2, d=2), func=ACT.Relu)
             return h[:].rearrange("c u p d -> c (u p d)").bitcast(F32)
 
-        def turn(a, b, hb):
+        hbs = {a: keep.tile([P, (b - a) * C, 4], BF16, align_bytes=64, name="hb_%d" % a) for a, b in BATCHES}
+
+        def turn(a, b, pairs):
             n = b - a
             ht = psum_t.tile([P, n, 2, C], F32, name="ht")
-            for e in range(a, b):
-                pairs = first_layer(e)
+            for i in range(n):
                 for u in range(2):
-                    nc.tensor.transpose(ht[:, e - a, u, :], pairs[:, u * P : (u + 1) * P], ident[:])
-            copy = nc.vector.tensor_copy if a in VECTOR_TURNS else nc.scalar.copy
-            copy(
+                    nc.tensor.transpose(ht[:, i, u, :], pairs[i][:, u * P : (u + 1) * P], ident[:])
+            first = max(lo for lo, hi in BATCHES if lo <= a)
+            hb = hbs[first][:, (a - first) * C : (b - first) * C, :]
+            nc.scalar.copy(
                 out=hb.rearrange("p c d -> p (c d)").bitcast(F32).rearrange("p (g c u) -> p g c u", g=n, u=2),
                 in_=ht[:].rearrange("p g u c -> p g c u"),
             )
 
-        def second_layer(a, b, hb):
+        waiting = None
+        for a, b in TURNS:
+            pairs = [first_layer(e) for e in range(a, b)]
+            if waiting is not None:
+                turn(*waiting)
+            waiting = (a, b, pairs)
+        turn(*waiting)
+
+        for i, (a, b) in enumerate(BATCHES):
             n = b - a
-            hw = keep.tile([P, n * C], U32, align_bytes=64, name="hw_%d" % a)
+            tag = "gw_1_%d" % CHUNKS[-2][0] if i == 0 else "hw_%d" % a
+            hw = keep.tile([P, n * C], U32, align_bytes=64, name="hw", tag=tag)
             hs = keep.tile([P, n * C], U8, align_bytes=64, name="hs_%d" % a)
-            nc.vector.quantize_mx(out=hw[:].bitcast(FP8X4), scales=hs[:], in_=hb[:].rearrange("p c d -> p (c d)"))
+            nc.vector.quantize_mx(out=hw[:].bitcast(FP8X4), scales=hs[:], in_=hbs[a][:].rearrange("p c d -> p (c d)"))
             y = psum_y.tile([N, n * C], F32, name="y")
             for e in range(a, b):
                 cols = slice((e - a) * C, (e - a + 1) * C)
@@ -215,18 +202,6 @@ def tile_moe_tk_mlp_relu_kernel(tc, xT, w1_words, w1_scales, w2_words, w2_scales
                     stop=True,
                 )
             nc.scalar.copy(out=y_all[:, a * C : b * C], in_=y[:])
-
-        gathered = 4
-        for i, (a, b) in enumerate(BATCHES):
-            hb = keep.tile([P, (b - a) * C, 4], BF16, align_bytes=64, name="hb_%d" % a)
-            for e in range(a, b, 2):
-                f = min(e + 2, b)
-                while gathered < len(CHUNKS) and CHUNKS[gathered - 4][1] <= e:
-                    gather_words(0, gathered)
-                    gather_words(1, gathered)
-                    gathered += 1
-                turn(e, f, hb[:, (e - a) * C : (f - a) * C, :])
-            second_layer(a, b, hb)
 
         for a, b in OUT_PARTS:
             prods = []

@@ -24,9 +24,12 @@ FLOPS = 2 * S * H * (K + N)
 
 SCALE_RUNS = ((0, 3), (3, 9), (9, 15))
 W_LOADS = (((0, 1), (1, 2)), ((2, 4),), ((4, 7), (7, 9)), ((9, 12), (12, 15)))
-EARLY = 2
-CHUNKS = ((2, 4), (4, 7), (7, 10), (10, 13), (13, 15))
-X_PARTS = (((0, 256, "v"), (256, 384, "v"), (384, 640, "s")), ((0, 256, "v"), (256, 512, "s"), (512, 640, "s")))
+EARLY = 6
+EARLY_CHUNKS = (((0, 3), (3, 6)), ((0, 1), (1, 2), (2, 4), (4, 6)))
+CHUNKS = ((6, 9), (9, 12), (12, 14), (14, 15))
+Y_ON_VECTOR = 2
+BANKS = 4
+X_PARTS = (((0, 256, "v"), (256, 384, "v"), (384, 640, "s")), ((0, 256, "s"), (256, 512, "s"), (512, 640, "s")))
 TURNS = ((0, 2), (2, 4), (4, 6), (6, 8), (8, 10), (10, 12), (12, 14), (14, 15))
 BATCHES = ((0, 4), (4, 8), (8, 12), (12, 14), (14, 15))
 OUT_PARTS = ((0, 512), (512, 640))
@@ -38,7 +41,8 @@ def tile_moe_tk_mlp_relu_kernel(tc, xT, w1_words, w1_scales, w2_words, w2_scales
         lists = ctx.enter_context(tc.tile_pool(name="lists", bufs=1))
         keep = ctx.enter_context(tc.tile_pool(name="keep", bufs=1))
         ring = ctx.enter_context(tc.tile_pool(name="ring", bufs=4))
-        psum_a = ctx.enter_context(tc.psum_pool(name="psum_a", bufs=4))
+        turns = ctx.enter_context(tc.tile_pool(name="turns", bufs=1))
+        psum_a = ctx.enter_context(tc.psum_pool(name="psum_a", bufs=1))
         psum_t = ctx.enter_context(tc.psum_pool(name="psum_t", bufs=2))
         psum_y = ctx.enter_context(tc.psum_pool(name="psum_y", bufs=2))
 
@@ -97,7 +101,10 @@ def tile_moe_tk_mlp_relu_kernel(tc, xT, w1_words, w1_scales, w2_words, w2_scales
         gs = {}
 
         def interleave(s, a, b, engine):
-            xb = keep.tile([P, b - a, 4], BF16, align_bytes=64, name="xb", tag="xb_%d_%d" % (s, a))
+            if s == PASSES - 1 and b == T:
+                xb = turns.tile([P, b - a, 4], BF16, align_bytes=64, name="xb_last", offset=(E - EARLY) * C - 64)
+            else:
+                xb = keep.tile([P, b - a, 4], BF16, align_bytes=64, name="xb", tag="xb_%d_%d" % (s, a))
             copy = nc.vector.tensor_copy if engine == "v" else nc.scalar.copy
             copy(
                 out=xb[:].rearrange("p (c i) j -> p c j i", i=4),
@@ -127,13 +134,12 @@ def tile_moe_tk_mlp_relu_kernel(tc, xT, w1_words, w1_scales, w2_words, w2_scales
             scales = keep.tile([P, (b - a) * C], U8, align_bytes=64, name="scales", tag="gs_%d_%d" % (s, a))
             gather(s, a, b, words[:], scales[:])
 
-        quantise_x(0)
-        gather_fresh(0, 0, EARLY)
-        quantise_x(1)
-        for e in range(EARLY):
-            gather_fresh(1, e, e + 1)
-        late_w = keep.tile([P, (E - EARLY) * C], U32, align_bytes=64, name="late_w", tag="x_raw1")
-        late_s = keep.tile([P, (E - EARLY) * C], U8, align_bytes=64, name="late_s", tag="xb_1_0")
+        for s in range(PASSES):
+            quantise_x(s)
+            for a, b in EARLY_CHUNKS[s]:
+                gather_fresh(s, a, b)
+        late_s = turns.tile([P, (E - EARLY) * C], U8, align_bytes=64, name="late_s", offset=0)
+        late_w = turns.tile([P, (E - EARLY) * C], U32, align_bytes=64, name="late_w", offset=(E - EARLY) * C)
         for a, b in CHUNKS:
             cols = slice((a - EARLY) * C, (b - EARLY) * C)
             gather(0, a, b, late_w[:, cols], late_s[:, cols])
@@ -142,7 +148,7 @@ def tile_moe_tk_mlp_relu_kernel(tc, xT, w1_words, w1_scales, w2_words, w2_scales
         y_all = keep.tile([P, S], F32, name="y_all")
 
         def first_layer(e):
-            acc = psum_a.tile([C, H], F32, name="acc")
+            acc = psum_a.tile([C, H], F32, name="acc", tag="acc%d" % (e % BANKS))
             w, at = w1[e]
             g = [i for i, run in enumerate(SCALE_RUNS) if run[0] <= e < run[1]][0]
             for s in range(PASSES):
@@ -185,11 +191,13 @@ def tile_moe_tk_mlp_relu_kernel(tc, xT, w1_words, w1_scales, w2_words, w2_scales
 
         for i, (a, b) in enumerate(BATCHES):
             n = b - a
-            tag = "gw_1_%d" % CHUNKS[-2][0] if i == 0 else "hw_%d" % a
-            hw = keep.tile([P, n * C], U32, align_bytes=64, name="hw", tag=tag)
+            hw = keep.tile([P, n * C], U32, align_bytes=64, name="hw_%d" % a)
             hs = keep.tile([P, n * C], U8, align_bytes=64, name="hs_%d" % a)
             nc.vector.quantize_mx(out=hw[:].bitcast(FP8X4), scales=hs[:], in_=hbs[a][:].rearrange("p c d -> p (c d)"))
-            y = psum_y.tile([N, n * C], F32, name="y")
+            if i < 3:
+                y = psum_a.tile([N, n * C], F32, name="y", tag="acc%d" % ((E + i) % BANKS))
+            else:
+                y = psum_y.tile([N, n * C], F32, name="y")
             for e in range(a, b):
                 cols = slice((e - a) * C, (e - a + 1) * C)
                 nc.tensor.matmul_mx(
@@ -201,7 +209,8 @@ def tile_moe_tk_mlp_relu_kernel(tc, xT, w1_words, w1_scales, w2_words, w2_scales
                     start=True,
                     stop=True,
                 )
-            nc.scalar.copy(out=y_all[:, a * C : b * C], in_=y[:])
+            copy = nc.vector.tensor_copy if i < Y_ON_VECTOR else nc.scalar.copy
+            copy(out=y_all[:, a * C : b * C], in_=y[:])
 
         for a, b in OUT_PARTS:
             prods = []

@@ -22,8 +22,8 @@ S = E * C
 PASSES = K // 512
 FLOPS = 2 * S * H * (K + N)
 
-SCALE_RUNS = ((0, 3), (3, 9), (9, 15))
-W_LOADS = (((0, 1), (1, 2)), ((2, 4),), ((4, 7), (7, 9)), ((9, 12), (12, 15)))
+SCALE_RUNS = ((0, 5), (5, 10), (10, 15))
+W_LOADS = (((0, 1), (1, 2)), ((2, 5),), ((5, 7), (7, 10)), ((10, 13), (13, 15)))
 EARLY = 6
 EARLY_CHUNKS = (((0, 3), (3, 6)), ((0, 1), (1, 2), (2, 4), (4, 6)))
 CHUNKS = ((6, 9), (9, 12), (12, 14), (14, 15))
@@ -32,7 +32,9 @@ BANKS = 4
 X_PARTS = (((0, 256, "v"), (256, 384, "v"), (384, 640, "s")), ((0, 256, "s"), (256, 512, "s"), (512, 640, "s")))
 TURNS = ((0, 2), (2, 4), (4, 6), (6, 8), (8, 10), (10, 12), (12, 14), (14, 15))
 BATCHES = ((0, 4), (4, 8), (8, 12), (12, 14), (14, 15))
-OUT_PARTS = ((0, 512), (512, 640))
+OUT_PARTS = ((0, 256), (256, 384), (384, 512), (512, 640))
+SUMS_ON_TENSOR = 2
+TURNS_ON_VECTOR = 15
 
 
 def tile_moe_tk_mlp_relu_kernel(tc, xT, w1_words, w1_scales, w2_words, w2_scales, gate, offs, pos1, pos2, pos3, out):
@@ -176,7 +178,8 @@ def tile_moe_tk_mlp_relu_kernel(tc, xT, w1_words, w1_scales, w2_words, w2_scales
                     nc.tensor.transpose(ht[:, i, u, :], pairs[i][:, u * P : (u + 1) * P], ident[:])
             first = max(lo for lo, hi in BATCHES if lo <= a)
             hb = hbs[first][:, (a - first) * C : (b - first) * C, :]
-            nc.scalar.copy(
+            copy = nc.vector.tensor_copy if a >= TURNS_ON_VECTOR else nc.scalar.copy
+            copy(
                 out=hb.rearrange("p c d -> p (c d)").bitcast(F32).rearrange("p (g c u) -> p g c u", g=n, u=2),
                 in_=ht[:].rearrange("p g u c -> p g c u"),
             )
@@ -212,7 +215,7 @@ def tile_moe_tk_mlp_relu_kernel(tc, xT, w1_words, w1_scales, w2_words, w2_scales
             copy = nc.vector.tensor_copy if i < Y_ON_VECTOR else nc.scalar.copy
             copy(out=y_all[:, a * C : b * C], in_=y[:])
 
-        for a, b in OUT_PARTS:
+        def products(a, b):
             prods = []
             for r in range(TOP):
                 prod = keep.tile([N, b - a], F32, name="prod_%d_%d" % (a, r))
@@ -223,6 +226,26 @@ def tile_moe_tk_mlp_relu_kernel(tc, xT, w1_words, w1_scales, w2_words, w2_scales
                     op=MULT,
                 )
                 prods.append(prod)
+            return prods
+
+        for i, (a, b) in enumerate(OUT_PARTS[:SUMS_ON_TENSOR]):
+            prods = products(a, b)
+            blocks = [slice(c, c + P) for c in range(0, b - a, P)]
+            sums = psum_a.tile([P, b - a], F32, name="sums", tag="acc%d" % (2 * i))
+            for cols in blocks:
+                for r in range(TOP):
+                    nc.tensor.matmul(sums[:, cols], prods[r][:, cols], ident[:], is_transpose=True, start=(r == 0), stop=(r == TOP - 1))
+            turned = keep.tile([P, b - a], F32, name="turned_%d" % a)
+            nc.scalar.copy(out=turned[:], in_=sums[:])
+            back = psum_a.tile([P, b - a], F32, name="back", tag="acc%d" % (2 * i + 1))
+            for cols in blocks:
+                nc.tensor.transpose(back[:, cols], turned[:, cols], ident[:])
+            result = keep.tile([N, b - a], F32, name="result_%d" % a)
+            nc.scalar.copy(out=result[:], in_=back[:])
+            nc.scalar.dma_start(out=out[:, a:b], in_=result[:])
+
+        for a, b in OUT_PARTS[SUMS_ON_TENSOR:]:
+            prods = products(a, b)
             part = keep.tile([N, b - a], F32, name="part_%d" % a)
             nc.vector.tensor_tensor(out=part[:], in0=prods[0][:], in1=prods[1][:], op=ADD)
             result = keep.tile([N, b - a], F32, name="result_%d" % a)

@@ -23,16 +23,18 @@ PASSES = K // 512
 FLOPS = 2 * S * H * (K + N)
 
 SCALE_RUNS = ((0, 5), (5, 10), (10, 15))
-W_LOADS = (((0, 1), (1, 2)), ((2, 5),), ((5, 7), (7, 10)), ((10, 13), (13, 15)))
-EARLY = 6
-EARLY_CHUNKS = (((0, 3), (3, 6)), ((0, 1), (1, 2), (2, 4), (4, 6)))
-CHUNKS = ((6, 9), (9, 12), (12, 14), (14, 15))
+W_LOADS = (((0, 1),), ((1, 3), (3, 5)), ((5, 7), (7, 10)), ((10, 13), (13, 15)))
+EARLY = 5
+EARLY_CHUNKS = (((0, 5),), ((0, 1), (1, 3), (3, 5)))
+CHUNKS = ((5, 7), (7, 9), (9, 11), (11, 13), (13, 14), (14, 15))
+WINDOW = 896
 Y_ON_VECTOR = 2
-BANKS = 4
-X_PARTS = (((0, 256, "v"), (256, 384, "v"), (384, 640, "s")), ((0, 256, "s"), (256, 512, "s"), (512, 640, "s")))
+X_LOADS = (((0, 640),), ((0, 384), (384, 640)))
+BANKS = 3
+X_PARTS = (((0, 256, "v"), (256, 384, "v"), (384, 640, "s")), ((0, 256, "s"), (256, 384, "s"), (384, 512, "s"), (512, 640, "s")))
 TURNS = ((0, 2), (2, 4), (4, 6), (6, 8), (8, 10), (10, 12), (12, 14), (14, 15))
 BATCHES = ((0, 4), (4, 8), (8, 12), (12, 14), (14, 15))
-OUT_PARTS = ((0, 256), (256, 384), (384, 512), (512, 640))
+OUT_PARTS = ((0, 256), (256, 384), (384, 640))
 SUMS_ON_TENSOR = 2
 TURNS_ON_VECTOR = 15
 
@@ -53,19 +55,20 @@ def tile_moe_tk_mlp_relu_kernel(tc, xT, w1_words, w1_scales, w2_words, w2_scales
 
         w1s = [keep.tile([P, (b - a) * PASSES * H], U8, align_bytes=64, name="w1s_%d" % a) for a, b in SCALE_RUNS]
         w2s = keep.tile([P, E * N], U8, align_bytes=64, name="w2s")
-        xs = [keep.tile([P, T], U8, align_bytes=64, name="xs%d" % s) for s in range(PASSES)]
-        for t in w1s[:1] + xs + w1s[1:] + [w2s]:
+        xs = [keep.tile([P, WINDOW], U8, align_bytes=64, name="xs%d" % s) for s in range(PASSES)]
+        for t in xs:
             nc.vector.memset(t[:].bitcast(I32), 0)
         ident = keep.tile([P, P], F32, name="ident")
         make_identity(nc, ident[:])
 
         x_view = xT.rearrange("(s p j) t -> s p j t", p=P, j=4)
-        x_raw = [keep.tile([P, 4, T], F32, align_bytes=64, name="x_raw%d" % s, tag="x_raw%d" % s) for s in range(PASSES)]
-        nc.sync.dma_start(out=x_raw[0][:], in_=x_view[0])
-        nc.sync.dma_start(offs_t[:], offs)
-        for r, pos in enumerate((pos1, pos2, pos3)):
-            nc.sync.dma_start(pos_t[r][:], pos)
-        nc.sync.dma_start(out=x_raw[1][:], in_=x_view[1])
+        x_raw = {}
+        for s in range(PASSES):
+            for a, b in X_LOADS[s]:
+                x_raw[s, a] = keep.tile([P, 4, b - a], F32, align_bytes=64, name="x_raw_%d_%d" % (s, a))
+                nc.sync.dma_start(out=x_raw[s, a][:], in_=x_view[s, :, :, a:b])
+            if s == 0:
+                nc.sync.dma_start(offs_t[:], offs)
 
         w1 = {}
         w1_view = w1_words.rearrange("e s p b -> p e s b").bitcast(I32)
@@ -95,10 +98,13 @@ def tile_moe_tk_mlp_relu_kernel(tc, xT, w1_words, w1_scales, w2_words, w2_scales
             )
         w2 = keep.tile([P, E, 2 * N], U8, align_bytes=64, name="w2")
         nc.sync.dma_start(out=w2[:].bitcast(I32), in_=w2_words.rearrange("e s p b -> p (e s) b").bitcast(I32))
+        for r, pos in enumerate((pos1, pos2, pos3)):
+            nc.sync.dma_start(pos_t[r][:], pos)
         gates = keep.tile([P, TOP, T], F32, name="gates")
         nc.sync.dma_start(out=gates[:], in_=gate.rearrange("r n t -> n r t"))
 
-        xw = [keep.tile([P, T], U32, align_bytes=64, name="xw%d" % s) for s in range(PASSES)]
+        xw = [keep.tile([P, WINDOW if s == 0 else T], U32, align_bytes=64, name="xw%d" % s) for s in range(PASSES)]
+        nc.vector.memset(xw[0][:, T:].bitcast(I32), 0)
         gw = {}
         gs = {}
 
@@ -108,9 +114,10 @@ def tile_moe_tk_mlp_relu_kernel(tc, xT, w1_words, w1_scales, w2_words, w2_scales
             else:
                 xb = keep.tile([P, b - a, 4], BF16, align_bytes=64, name="xb", tag="xb_%d_%d" % (s, a))
             copy = nc.vector.tensor_copy if engine == "v" else nc.scalar.copy
+            first = max(lo for lo, hi in X_LOADS[s] if lo <= a)
             copy(
                 out=xb[:].rearrange("p (c i) j -> p c j i", i=4),
-                in_=x_raw[s][:, :, a:b].rearrange("p j (c i) -> p c j i", i=4),
+                in_=x_raw[s, first][:, :, a - first : b - first].rearrange("p j (c i) -> p c j i", i=4),
             )
             return xb
 
@@ -149,21 +156,31 @@ def tile_moe_tk_mlp_relu_kernel(tc, xT, w1_words, w1_scales, w2_words, w2_scales
 
         y_all = keep.tile([P, S], F32, name="y_all")
 
-        def first_layer(e):
-            acc = psum_a.tile([C, H], F32, name="acc", tag="acc%d" % (e % BANKS))
+        accs = {}
+
+        def one_pass(e, s):
+            if s == 0:
+                accs[e] = psum_a.tile([C, H], F32, name="acc", tag="acc%d" % (e % BANKS))
             w, at = w1[e]
             g = [i for i, run in enumerate(SCALE_RUNS) if run[0] <= e < run[1]][0]
-            for s in range(PASSES):
-                col = ((e - SCALE_RUNS[g][0]) * PASSES + s) * H
-                nc.tensor.matmul_mx(
-                    out=acc[:],
-                    lhsT=gw[s, e].bitcast(FP8X4),
-                    lhsT_scale=gs[s, e],
-                    rhs=w[:, at, s, :].bitcast(FP4X4),
-                    rhs_scale=w1s[g][:, col : col + H],
-                    start=(s == 0),
-                    stop=(s == PASSES - 1),
-                )
+            col = ((e - SCALE_RUNS[g][0]) * PASSES + s) * H
+            nc.tensor.matmul_mx(
+                out=accs[e][:],
+                lhsT=gw[s, e].bitcast(FP8X4),
+                lhsT_scale=gs[s, e],
+                rhs=w[:, at, s, :].bitcast(FP4X4),
+                rhs_scale=w1s[g][:, col : col + H],
+                start=(s == 0),
+                stop=(s == PASSES - 1),
+            )
+
+        for e in range(BANKS):
+            one_pass(e, 0)
+
+        def first_layer(e):
+            for s in range(1 if e < BANKS else 0, PASSES):
+                one_pass(e, s)
+            acc = accs[e]
             h = ring.tile([C, 2, P, 2], BF16, name="h")
             nc.scalar.activation(out=h[:], in_=acc[:].rearrange("c (p u d) -> c u p d", u=2, d=2), func=ACT.Relu)
             return h[:].rearrange("c u p d -> c (u p d)").bitcast(F32)
@@ -231,23 +248,26 @@ def tile_moe_tk_mlp_relu_kernel(tc, xT, w1_words, w1_scales, w2_words, w2_scales
         for i, (a, b) in enumerate(OUT_PARTS[:SUMS_ON_TENSOR]):
             prods = products(a, b)
             blocks = [slice(c, c + P) for c in range(0, b - a, P)]
-            sums = psum_a.tile([P, b - a], F32, name="sums", tag="acc%d" % (2 * i))
+            sums = psum_t.tile([P, b - a], F32, name="sums", tag="ht")
             for cols in blocks:
                 for r in range(TOP):
                     nc.tensor.matmul(sums[:, cols], prods[r][:, cols], ident[:], is_transpose=True, start=(r == 0), stop=(r == TOP - 1))
             turned = keep.tile([P, b - a], F32, name="turned_%d" % a)
             nc.scalar.copy(out=turned[:], in_=sums[:])
-            back = psum_a.tile([P, b - a], F32, name="back", tag="acc%d" % (2 * i + 1))
+            back = psum_a.tile([P, b - a], F32, name="back", tag="acc%d" % i)
             for cols in blocks:
                 nc.tensor.transpose(back[:, cols], turned[:, cols], ident[:])
             result = keep.tile([N, b - a], F32, name="result_%d" % a)
             nc.scalar.copy(out=result[:], in_=back[:])
-            nc.scalar.dma_start(out=out[:, a:b], in_=result[:])
+            queue = nc.scalar if i == SUMS_ON_TENSOR - 1 else nc.sync
+            queue.dma_start(out=out[:, a:b], in_=result[:])
 
         for a, b in OUT_PARTS[SUMS_ON_TENSOR:]:
             prods = products(a, b)
-            part = keep.tile([N, b - a], F32, name="part_%d" % a)
-            nc.vector.tensor_tensor(out=part[:], in0=prods[0][:], in1=prods[1][:], op=ADD)
-            result = keep.tile([N, b - a], F32, name="result_%d" % a)
-            nc.vector.tensor_tensor(out=result[:], in0=part[:], in1=prods[2][:], op=ADD)
-            nc.sync.dma_start(out=out[:, a:b], in_=result[:])
+            for c in range(0, b - a, P):
+                cols = slice(c, c + P)
+                part = keep.tile([N, P], F32, name="part_%d" % (a + c))
+                nc.vector.tensor_tensor(out=part[:], in0=prods[0][:, cols], in1=prods[1][:, cols], op=ADD)
+                result = keep.tile([N, P], F32, name="result_%d" % (a + c))
+                nc.vector.tensor_tensor(out=result[:], in0=part[:], in1=prods[2][:, cols], op=ADD)
+                nc.sync.dma_start(out=out[:, a + c : a + c + P], in_=result[:])

@@ -174,11 +174,8 @@ def tile_moe_tk_mlp_relu_kernel(tc, xT, w1_words, w1_scales, w2_words, w2_scales
                 stop=(s == PASSES - 1),
             )
 
-        for e in range(BANKS):
-            one_pass(e, 0)
-
         def first_layer(e):
-            for s in range(1 if e < BANKS else 0, PASSES):
+            for s in range(PASSES):
                 one_pass(e, s)
             acc = accs[e]
             h = ring.tile([C, 2, P, 2], BF16, name="h")
@@ -264,10 +261,13 @@ def tile_moe_tk_mlp_relu_kernel(tc, xT, w1_words, w1_scales, w2_words, w2_scales
 
         for a, b in OUT_PARTS[SUMS_ON_TENSOR:]:
             prods = products(a, b)
-            for c in range(0, b - a, P):
-                cols = slice(c, c + P)
-                part = keep.tile([N, P], F32, name="part_%d" % (a + c))
+            halves = [slice(c, c + P) for c in range(0, b - a, P)]
+            parts = []
+            for cols in halves:
+                part = keep.tile([N, P], F32, name="part_%d" % (a + cols.start))
                 nc.vector.tensor_tensor(out=part[:], in0=prods[0][:, cols], in1=prods[1][:, cols], op=ADD)
-                result = keep.tile([N, P], F32, name="result_%d" % (a + c))
+                parts.append(part)
+            for cols, part in zip(halves, parts):
+                result = keep.tile([N, P], F32, name="result_%d" % (a + cols.start))
                 nc.vector.tensor_tensor(out=result[:], in0=part[:], in1=prods[2][:, cols], op=ADD)
-                nc.sync.dma_start(out=out[:, a + c : a + c + P], in_=result[:])
+                nc.sync.dma_start(out=out[:, a + cols.start : a + cols.stop], in_=result[:])

@@ -24,14 +24,14 @@ FLOPS = 2 * S * H * (K + N)
 
 SCALE_RUNS = ((0, 5), (5, 10), (10, 15))
 W_LOADS = (((0, 1),), ((1, 3), (3, 5)), ((5, 7), (7, 10)), ((10, 13), (13, 15)))
-EARLY = 5
-EARLY_CHUNKS = (((0, 5),), ((0, 1), (1, 3), (3, 5)))
-CHUNKS = ((5, 7), (7, 9), (9, 11), (11, 13), (13, 14), (14, 15))
-WINDOW = 896
+EARLY = 7
+EARLY_CHUNKS = (((0, 4), (4, 7)), ((0, 1), (1, 3), (3, 5), (5, 7)))
+CHUNKS = ((7, 9), (9, 11), (11, 13), (13, 14), (14, 15))
+WINDOW = 704
 Y_ON_VECTOR = 2
-X_LOADS = (((0, 640),), ((0, 384), (384, 640)))
+X_LOADS = (((0, 640),), ((0, 640),))
 BANKS = 3
-X_PARTS = (((0, 256, "v"), (256, 384, "v"), (384, 640, "s")), ((0, 256, "s"), (256, 384, "s"), (384, 512, "s"), (512, 640, "s")))
+X_PARTS = (((0, 256, "v"), (256, 384, "v"), (384, 640, "s")), ((0, 256, "s"), (256, 512, "s"), (512, 640, "s")))
 TURNS = ((0, 2), (2, 4), (4, 6), (6, 8), (8, 10), (10, 12), (12, 14), (14, 15))
 BATCHES = ((0, 4), (4, 8), (8, 12), (12, 14), (14, 15))
 OUT_PARTS = ((0, 256), (256, 384), (384, 640))

@@ -36,6 +36,7 @@ TURNS = ((0, 2), (2, 4), (4, 6), (6, 8), (8, 10), (10, 12), (12, 14), (14, 15))
 BATCHES = ((0, 4), (4, 8), (8, 12), (12, 14), (14, 15))
 OUT_PARTS = ((0, 256), (256, 384), (384, 640))
 SUMS_ON_TENSOR = 2
+ON_SCALAR = (1, 1, 2)
 TURNS_ON_VECTOR = 15
 
 
@@ -229,16 +230,21 @@ def tile_moe_tk_mlp_relu_kernel(tc, xT, w1_words, w1_scales, w2_words, w2_scales
             copy = nc.vector.tensor_copy if i < Y_ON_VECTOR else nc.scalar.copy
             copy(out=y_all[:, a * C : b * C], in_=y[:])
 
+        fetched = {}
+        for i, (a, b) in enumerate(OUT_PARTS):
+            for r in range(TOP - ON_SCALAR[i], TOP):
+                fetched[a, r] = keep.tile([N, b - a], F32, name="fetched_%d_%d" % (a, r))
+                nc.scalar.activation(out=fetched[a, r][:], in_=y_all[:].indirect(pos_t[r][:, a // 16 : b // 16]), func=ACT.Copy)
+
         def products(a, b):
             prods = []
             for r in range(TOP):
                 prod = keep.tile([N, b - a], F32, name="prod_%d_%d" % (a, r))
-                nc.vector.tensor_tensor(
-                    out=prod[:],
-                    in0=y_all[:].indirect(pos_t[r][:, a // 16 : b // 16]),
-                    in1=gates[:, r, a:b],
-                    op=MULT,
-                )
+                if (a, r) in fetched:
+                    values = fetched[a, r][:]
+                else:
+                    values = y_all[:].indirect(pos_t[r][:, a // 16 : b // 16])
+                nc.vector.tensor_tensor(out=prod[:], in0=values, in1=gates[:, r, a:b], op=MULT)
                 prods.append(prod)
             return prods
 

@@ -23,9 +23,9 @@ PASSES = K // 512
 FLOPS = 2 * S * H * (K + N)
 
 SCALE_RUNS = ((0, 5), (5, 10), (10, 15))
-W_LOADS = (((0, 1),), ((1, 3), (3, 5)), ((5, 7), (7, 10)), ((10, 13), (13, 15)))
+W_LOADS = (((0, 1),), ((1, 2), (2, 3), (3, 5)), ((5, 7), (7, 10)), ((10, 13), (13, 14), (14, 15)))
 EARLY = 7
-EARLY_CHUNKS = (((0, 4), (4, 7)), ((0, 1), (1, 3), (3, 5), (5, 7)))
+EARLY_CHUNKS = (((0, 4), (4, 7)), ((0, 1), (1, 2), (2, 3), (3, 5), (5, 7)))
 CHUNKS = ((7, 9), (9, 11), (11, 13), (13, 14), (14, 15))
 WINDOW = 704
 Y_ON_VECTOR = 2

@@ -25,7 +25,7 @@ FLOPS = 2 * S * H * (K + N)
 SCALE_RUNS = ((0, 5), (5, 10), (10, 15))
 W_LOADS = (((0, 1),), ((1, 2), (2, 3), (3, 5)), ((5, 7), (7, 10)), ((10, 13), (13, 14), (14, 15)))
 EARLY = 7
-EARLY_CHUNKS = (((0, 4), (4, 7)), ((0, 1), (1, 2), (2, 3), (3, 5), (5, 7)))
+EARLY_CHUNKS = (((0, 4), (4, 7)), ((0, 1), (1, 3), (3, 5), (5, 7)))
 CHUNKS = ((7, 9), (9, 11), (11, 13), (13, 14), (14, 15))
 WINDOW = 704
 Y_ON_VECTOR = 2
@@ -36,7 +36,7 @@ TURNS = ((0, 2), (2, 4), (4, 6), (6, 8), (8, 10), (10, 12), (12, 14), (14, 15))
 BATCHES = ((0, 4), (4, 8), (8, 12), (12, 14), (14, 15))
 OUT_PARTS = ((0, 256), (256, 384), (384, 640))
 SUMS_ON_TENSOR = 2
-ON_SCALAR = (1, 1, 2)
+ON_SCALAR = (1, 2, 2)
 TURNS_ON_VECTOR = 15
 
 

@@ -25,8 +25,6 @@ FLOPS = 2 * S * H * (K + N)
 SCALE_RUNS = ((0, 5), (5, 10), (10, 15))
 W_LOADS = (((0, 1),), ((1, 2), (2, 3), (3, 5)), ((5, 7), (7, 10)), ((10, 13), (13, 14), (14, 15)))
 EARLY = 7
-EARLY_CHUNKS = (((0, 4), (4, 7)), ((0, 1), (1, 3), (3, 5), (5, 7)))
-CHUNKS = ((7, 9), (9, 11), (11, 13), (13, 14), (14, 15))
 WINDOW = 704
 Y_ON_VECTOR = 2
 X_LOADS = (((0, 640),), ((0, 640),))
@@ -131,29 +129,52 @@ def tile_moe_tk_mlp_relu_kernel(tc, xT, w1_words, w1_scales, w2_words, w2_scales
                     in_=xb[:].rearrange("p t j -> p (t j)"),
                 )
 
-        def gather(s, a, b, words, scales):
-            picks = offs_t[:, a * C // 16 : b * C // 16]
-            nc.vector.tensor_copy(out=scales, in_=xs[s][:].indirect(picks))
-            nc.vector.tensor_copy(out=words, in_=xw[s][:].indirect(picks))
+        def picks(a, b):
+            return offs_t[:, a * C // 16 : b * C // 16]
+
+        def gather_bytes(s, a, b):
+            if s == 0 and a >= EARLY:
+                scales = late_s[:, (a - EARLY) * C : (b - EARLY) * C]
+            else:
+                scales = keep.tile([P, (b - a) * C], U8, align_bytes=64, name="gs_%d_%d" % (s, a))[:]
+            nc.vector.tensor_copy(out=scales, in_=xs[s][:].indirect(picks(a, b)))
             for e in range(a, b):
-                gw[s, e] = words[:, (e - a) * C : (e - a + 1) * C]
                 gs[s, e] = scales[:, (e - a) * C : (e - a + 1) * C]
 
-        def gather_fresh(s, a, b):
-            words = keep.tile([P, (b - a) * C], U32, align_bytes=64, name="words", tag="gw_%d_%d" % (s, a))
-            scales = keep.tile([P, (b - a) * C], U8, align_bytes=64, name="scales", tag="gs_%d_%d" % (s, a))
-            gather(s, a, b, words[:], scales[:])
+        def gather_words(s, a, b):
+            if s == 0 and a >= EARLY:
+                words = late_w[:, (a - EARLY) * C : (b - EARLY) * C]
+            else:
+                words = keep.tile([P, (b - a) * C], U32, align_bytes=64, name="gw_%d_%d" % (s, a))[:]
+            nc.vector.tensor_copy(out=words, in_=xw[s][:].indirect(picks(a, b)))
+            for e in range(a, b):
+                gw[s, e] = words[:, (e - a) * C : (e - a + 1) * C]
 
-        for s in range(PASSES):
-            quantise_x(s)
-            for a, b in EARLY_CHUNKS[s]:
-                gather_fresh(s, a, b)
+        def gather(s, a, b):
+            gather_bytes(s, a, b)
+            gather_words(s, a, b)
+
+        quantise_x(0)
+        gather(0, 0, 4)
+        gather(0, 4, EARLY)
+        quantise_x(1)
         late_s = turns.tile([P, (E - EARLY) * C], U8, align_bytes=64, name="late_s", offset=0)
         late_w = turns.tile([P, (E - EARLY) * C], U32, align_bytes=64, name="late_w", offset=(E - EARLY) * C)
-        for a, b in CHUNKS:
-            cols = slice((a - EARLY) * C, (b - EARLY) * C)
-            gather(0, a, b, late_w[:, cols], late_s[:, cols])
-            gather_fresh(1, a, b)
+        gather(1, 0, 1)
+        gather(1, 1, 3)
+        gather_bytes(1, 3, 7)
+        gather_words(1, 3, 5)
+        gather_words(1, 5, 7)
+        gather(0, 7, 11)
+        gather_bytes(1, 7, 11)
+        gather_words(1, 7, 9)
+        gather_words(1, 9, 11)
+        gather_bytes(0, 11, 15)
+        gather_words(0, 11, 13)
+        gather(1, 11, 13)
+        gather_words(0, 13, 15)
+        gather(1, 13, 14)
+        gather(1, 14, 15)
 
         y_all = keep.tile([P, S], F32, name="y_all")
 

@@ -99,8 +99,10 @@ def tile_moe_tk_mlp_relu_kernel(tc, xT, w1_words, w1_scales, w2_words, w2_scales
         nc.sync.dma_start(out=w2[:].bitcast(I32), in_=w2_words.rearrange("e s p b -> p (e s) b").bitcast(I32))
         for r, pos in enumerate((pos1, pos2, pos3)):
             nc.sync.dma_start(pos_t[r][:], pos)
-        gates = keep.tile([P, TOP, T], F32, name="gates")
-        nc.sync.dma_start(out=gates[:], in_=gate.rearrange("r n t -> n r t"))
+        gates = {}
+        for a, b in OUT_PARTS:
+            gates[a] = keep.tile([P, TOP, b - a], F32, name="gates_%d" % a)
+            nc.sync.dma_start(out=gates[a][:], in_=gate.rearrange("r n t -> n r t")[:, :, a:b])
 
         xw = [keep.tile([P, WINDOW if s == 0 else T], U32, align_bytes=64, name="xw%d" % s) for s in range(PASSES)]
         nc.vector.memset(xw[0][:, T:].bitcast(I32), 0)
@@ -265,7 +267,7 @@ def tile_moe_tk_mlp_relu_kernel(tc, xT, w1_words, w1_scales, w2_words, w2_scales
                     values = fetched[a, r][:]
                 else:
                     values = y_all[:].indirect(pos_t[r][:, a // 16 : b // 16])
-                nc.vector.tensor_tensor(out=prod[:], in0=values, in1=gates[:, r, a:b], op=MULT)
+                nc.vector.tensor_tensor(out=prod[:], in0=values, in1=gates[a][:, r, :], op=MULT)
                 prods.append(prod)
             return prods
 

from contextlib import ExitStack

import concourse.mybir as mybir
from concourse.masks import make_identity

F32 = mybir.dt.float32
BF16 = mybir.dt.bfloat16
I32 = mybir.dt.int32
U32 = mybir.dt.uint32
U16 = mybir.dt.uint16
U8 = mybir.dt.uint8
FP8X4 = mybir.dt.float8_e4m3fn_x4
FP4X4 = mybir.dt.float4_e2m1fn_x4
ACT = mybir.ActivationFunctionType
MULT = mybir.AluOpType.mult
ADD = mybir.AluOpType.add

P = 128
K, T, E, C, H, N = 1024, 640, 15, 128, 512, 128
TOP = 3
S = E * C
PASSES = K // 512
FLOPS = 2 * S * H * (K + N)

SCALE_RUNS = ((0, 5), (5, 10), (10, 15))
W_LOADS = (((0, 1),), ((1, 2), (2, 3), (3, 5)), ((5, 7), (7, 10)), ((10, 13), (13, 14), (14, 15)))
EARLY = 7
WINDOW = 704
Y_ON_VECTOR = 2
X_LOADS = (((0, 640),), ((0, 640),))
BANKS = 3
X_PARTS = (((0, 256, "v"), (256, 384, "v"), (384, 640, "s")), ((0, 256, "s"), (256, 512, "s"), (512, 640, "s")))
TURNS = ((0, 2), (2, 4), (4, 6), (6, 8), (8, 10), (10, 12), (12, 14), (14, 15))
BATCHES = ((0, 4), (4, 8), (8, 12), (12, 14), (14, 15))
OUT_PARTS = ((0, 256), (256, 384), (384, 640))
SUMS_ON_TENSOR = 2
ON_SCALAR = (1, 2, 2)
TURNS_ON_VECTOR = 15


def tile_moe_tk_mlp_relu_kernel(tc, xT, w1_words, w1_scales, w2_words, w2_scales, gate, offs, pos1, pos2, pos3, out):
    nc = tc.nc
    with ExitStack() as ctx:
        lists = ctx.enter_context(tc.tile_pool(name="lists", bufs=1))
        keep = ctx.enter_context(tc.tile_pool(name="keep", bufs=1))
        ring = ctx.enter_context(tc.tile_pool(name="ring", bufs=4))
        turns = ctx.enter_context(tc.tile_pool(name="turns", bufs=1))
        psum_a = ctx.enter_context(tc.psum_pool(name="psum_a", bufs=1))
        psum_t = ctx.enter_context(tc.psum_pool(name="psum_t", bufs=2))
        psum_y = ctx.enter_context(tc.psum_pool(name="psum_y", bufs=2))

        offs_t = lists.tile([P, S // 16], U16, name="offs_t")
        pos_t = [lists.tile([P, T // 16], U16, name="pos_t%d" % r) for r in range(TOP)]

        w1s = [keep.tile([P, (b - a) * PASSES * H], U8, align_bytes=64, name="w1s_%d" % a) for a, b in SCALE_RUNS]
        w2s = keep.tile([P, E * N], U8, align_bytes=64, name="w2s")
        xs = [keep.tile([P, WINDOW], U8, align_bytes=64, name="xs%d" % s) for s in range(PASSES)]
        for t in xs:
            nc.vector.memset(t[:].bitcast(I32), 0)
        ident = keep.tile([P, P], F32, name="ident")
        make_identity(nc, ident[:])

        x_view = xT.rearrange("(s p j) t -> s p j t", p=P, j=4)
        x_raw = {}
        for s in range(PASSES):
            for a, b in X_LOADS[s]:
                x_raw[s, a] = keep.tile([P, 4, b - a], F32, align_bytes=64, name="x_raw_%d_%d" % (s, a))
                nc.sync.dma_start(out=x_raw[s, a][:], in_=x_view[s, :, :, a:b])
            if s == 0:
                nc.sync.dma_start(offs_t[:], offs)

        w1 = {}
        w1_view = w1_words.rearrange("e s p b -> p e s b").bitcast(I32)
        w1s_view = w1_scales.rearrange("e s (q r) i -> r q (e s) i", r=4).bitcast(I32)
        w2s_view = w2_scales.rearrange("e s (q r) n -> r q (e s) n", r=4).bitcast(I32)

        def load_w1(a, b):
            w = keep.tile([P, b - a, PASSES, 2 * H], U8, align_bytes=64, name="w1_%d" % a)
            nc.sync.dma_start(out=w[:].bitcast(I32), in_=w1_view[:, a:b])
            for e in range(a, b):
                w1[e] = (w, e - a)

        for a, b in W_LOADS[0]:
            load_w1(a, b)
        for g, (lo, hi) in enumerate(SCALE_RUNS):
            for r in range(4):
                nc.sync.dma_start(
                    out=w1s[g][r:P:32, :].bitcast(I32).rearrange("q (a i) -> q a i", i=H // 4),
                    in_=w1s_view[r, :, lo * PASSES : hi * PASSES, :],
                )
            for a, b in W_LOADS[g + 1]:
                load_w1(a, b)
        for r in range(4):
            nc.sync.dma_start(
                out=w2s[r:P:32, :].bitcast(I32).rearrange("q (a n) -> q a n", n=N // 4),
                in_=w2s_view[r],
            )
        w2 = keep.tile([P, E, 2 * N], U8, align_bytes=64, name="w2")
        nc.sync.dma_start(out=w2[:].bitcast(I32), in_=w2_words.rearrange("e s p b -> p (e s) b").bitcast(I32))
        for r, pos in enumerate((pos1, pos2, pos3)):
            nc.sync.dma_start(pos_t[r][:], pos)
        gates = {}
        for a, b in OUT_PARTS:
            gates[a] = keep.tile([P, TOP, b - a], F32, name="gates_%d" % a)
            nc.sync.dma_start(out=gates[a][:], in_=gate.rearrange("r n t -> n r t")[:, :, a:b])

        xw = [keep.tile([P, WINDOW if s == 0 else T], U32, align_bytes=64, name="xw%d" % s) for s in range(PASSES)]
        nc.vector.memset(xw[0][:, T:].bitcast(I32), 0)
        gw = {}
        gs = {}

        def interleave(s, a, b, engine):
            if s == PASSES - 1 and b == T:
                xb = turns.tile([P, b - a, 4], BF16, align_bytes=64, name="xb_last", offset=(E - EARLY) * C - 64)
            else:
                xb = keep.tile([P, b - a, 4], BF16, align_bytes=64, name="xb", tag="xb_%d_%d" % (s, a))
            copy = nc.vector.tensor_copy if engine == "v" else nc.scalar.copy
            first = max(lo for lo, hi in X_LOADS[s] if lo <= a)
            copy(
                out=xb[:].rearrange("p (c i) j -> p c j i", i=4),
                in_=x_raw[s, first][:, :, a - first : b - first].rearrange("p j (c i) -> p c j i", i=4),
            )
            return xb

        def quantise_x(s):
            xbs = [interleave(s, a, b, engine) for a, b, engine in X_PARTS[s]]
            for xb, (a, b, engine) in zip(xbs, X_PARTS[s]):
                nc.vector.quantize_mx(
                    out=xw[s][:, a:b].bitcast(FP8X4),
                    scales=xs[s][:, a:b],
                    in_=xb[:].rearrange("p t j -> p (t j)"),
                )

        def picks(a, b):
            return offs_t[:, a * C // 16 : b * C // 16]

        def gather_bytes(s, a, b):
            if s == 0 and a >= EARLY:
                scales = late_s[:, (a - EARLY) * C : (b - EARLY) * C]
            else:
                scales = keep.tile([P, (b - a) * C], U8, align_bytes=64, name="gs_%d_%d" % (s, a))[:]
            nc.vector.tensor_copy(out=scales, in_=xs[s][:].indirect(picks(a, b)))
            for e in range(a, b):
                gs[s, e] = scales[:, (e - a) * C : (e - a + 1) * C]

        def gather_words(s, a, b):
            if s == 0 and a >= EARLY:
                words = late_w[:, (a - EARLY) * C : (b - EARLY) * C]
            else:
                words = keep.tile([P, (b - a) * C], U32, align_bytes=64, name="gw_%d_%d" % (s, a))[:]
            nc.vector.tensor_copy(out=words, in_=xw[s][:].indirect(picks(a, b)))
            for e in range(a, b):
                gw[s, e] = words[:, (e - a) * C : (e - a + 1) * C]

        def gather(s, a, b):
            gather_bytes(s, a, b)
            gather_words(s, a, b)

        quantise_x(0)
        gather(0, 0, 4)
        gather(0, 4, EARLY)
        quantise_x(1)
        late_s = turns.tile([P, (E - EARLY) * C], U8, align_bytes=64, name="late_s", offset=0)
        late_w = turns.tile([P, (E - EARLY) * C], U32, align_bytes=64, name="late_w", offset=(E - EARLY) * C)
        gather(1, 0, 1)
        gather(1, 1, 3)
        gather_bytes(1, 3, 7)
        gather_words(1, 3, 5)
        gather_words(1, 5, 7)
        gather(0, 7, 11)
        gather_bytes(1, 7, 11)
        gather_words(1, 7, 9)
        gather_words(1, 9, 11)
        gather_bytes(0, 11, 15)
        gather_words(0, 11, 13)
        gather(1, 11, 13)
        gather_words(0, 13, 15)
        gather(1, 13, 14)
        gather(1, 14, 15)

        y_all = keep.tile([P, S], F32, name="y_all")

        accs = {}

        def one_pass(e, s):
            if s == 0:
                accs[e] = psum_a.tile([C, H], F32, name="acc", tag="acc%d" % (e % BANKS))
            w, at = w1[e]
            g = [i for i, run in enumerate(SCALE_RUNS) if run[0] <= e < run[1]][0]
            col = ((e - SCALE_RUNS[g][0]) * PASSES + s) * H
            nc.tensor.matmul_mx(
                out=accs[e][:],
                lhsT=gw[s, e].bitcast(FP8X4),
                lhsT_scale=gs[s, e],
                rhs=w[:, at, s, :].bitcast(FP4X4),
                rhs_scale=w1s[g][:, col : col + H],
                start=(s == 0),
                stop=(s == PASSES - 1),
            )

        def first_layer(e):
            for s in range(PASSES):
                one_pass(e, s)
            acc = accs[e]
            h = ring.tile([C, 2, P, 2], BF16, name="h")
            nc.scalar.activation(out=h[:], in_=acc[:].rearrange("c (p u d) -> c u p d", u=2, d=2), func=ACT.Relu)
            return h[:].rearrange("c u p d -> c (u p d)").bitcast(F32)

        hbs = {a: keep.tile([P, (b - a) * C, 4], BF16, align_bytes=64, name="hb_%d" % a) for a, b in BATCHES}

        def turn(a, b, pairs):
            n = b - a
            ht = psum_t.tile([P, n, 2, C], F32, name="ht")
            for i in range(n):
                for u in range(2):
                    nc.tensor.transpose(ht[:, i, u, :], pairs[i][:, u * P : (u + 1) * P], ident[:])
            first = max(lo for lo, hi in BATCHES if lo <= a)
            hb = hbs[first][:, (a - first) * C : (b - first) * C, :]
            copy = nc.vector.tensor_copy if a >= TURNS_ON_VECTOR else nc.scalar.copy
            copy(
                out=hb.rearrange("p c d -> p (c d)").bitcast(F32).rearrange("p (g c u) -> p g c u", g=n, u=2),
                in_=ht[:].rearrange("p g u c -> p g c u"),
            )

        waiting = None
        for a, b in TURNS:
            pairs = [first_layer(e) for e in range(a, b)]
            if waiting is not None:
                turn(*waiting)
            waiting = (a, b, pairs)
        turn(*waiting)

        for i, (a, b) in enumerate(BATCHES):
            n = b - a
            hw = keep.tile([P, n * C], U32, align_bytes=64, name="hw_%d" % a)
            hs = keep.tile([P, n * C], U8, align_bytes=64, name="hs_%d" % a)
            nc.vector.quantize_mx(out=hw[:].bitcast(FP8X4), scales=hs[:], in_=hbs[a][:].rearrange("p c d -> p (c d)"))
            if i < 3:
                y = psum_a.tile([N, n * C], F32, name="y", tag="acc%d" % ((E + i) % BANKS))
            else:
                y = psum_y.tile([N, n * C], F32, name="y")
            for e in range(a, b):
                cols = slice((e - a) * C, (e - a + 1) * C)
                nc.tensor.matmul_mx(
                    out=y[:, cols],
                    lhsT=w2[:, e, :].bitcast(FP4X4),
                    lhsT_scale=w2s[:, e * N : (e + 1) * N],
                    rhs=hw[:, cols].bitcast(FP8X4),
                    rhs_scale=hs[:, cols],
                    start=True,
                    stop=True,
                )
            copy = nc.vector.tensor_copy if i < Y_ON_VECTOR else nc.scalar.copy
            copy(out=y_all[:, a * C : b * C], in_=y[:])

        fetched = {}
        for i, (a, b) in enumerate(OUT_PARTS):
            for r in range(TOP - ON_SCALAR[i], TOP):
                fetched[a, r] = keep.tile([N, b - a], F32, name="fetched_%d_%d" % (a, r))
                nc.scalar.activation(out=fetched[a, r][:], in_=y_all[:].indirect(pos_t[r][:, a // 16 : b // 16]), func=ACT.Copy)

        def products(a, b):
            prods = []
            for r in range(TOP):
                prod = keep.tile([N, b - a], F32, name="prod_%d_%d" % (a, r))
                if (a, r) in fetched:
                    values = fetched[a, r][:]
                else:
                    values = y_all[:].indirect(pos_t[r][:, a // 16 : b // 16])
                nc.vector.tensor_tensor(out=prod[:], in0=values, in1=gates[a][:, r, :], op=MULT)
                prods.append(prod)
            return prods

        for i, (a, b) in enumerate(OUT_PARTS[:SUMS_ON_TENSOR]):
            prods = products(a, b)
            blocks = [slice(c, c + P) for c in range(0, b - a, P)]
            sums = psum_t.tile([P, b - a], F32, name="sums", tag="ht")
            for cols in blocks:
                for r in range(TOP):
                    nc.tensor.matmul(sums[:, cols], prods[r][:, cols], ident[:], is_transpose=True, start=(r == 0), stop=(r == TOP - 1))
            turned = keep.tile([P, b - a], F32, name="turned_%d" % a)
            nc.scalar.copy(out=turned[:], in_=sums[:])
            back = psum_a.tile([P, b - a], F32, name="back", tag="acc%d" % i)
            for cols in blocks:
                nc.tensor.transpose(back[:, cols], turned[:, cols], ident[:])
            result = keep.tile([N, b - a], F32, name="result_%d" % a)
            nc.scalar.copy(out=result[:], in_=back[:])
            queue = nc.scalar if i == SUMS_ON_TENSOR - 1 else nc.sync
            queue.dma_start(out=out[:, a:b], in_=result[:])

        for a, b in OUT_PARTS[SUMS_ON_TENSOR:]:
            prods = products(a, b)
            halves = [slice(c, c + P) for c in range(0, b - a, P)]
            parts = []
            for cols in halves:
                part = keep.tile([N, P], F32, name="part_%d" % (a + cols.start))
                nc.vector.tensor_tensor(out=part[:], in0=prods[0][:, cols], in1=prods[1][:, cols], op=ADD)
                parts.append(part)
            for cols, part in zip(halves, parts):
                result = keep.tile([N, P], F32, name="result_%d" % (a + cols.start))
                nc.vector.tensor_tensor(out=result[:], in0=part[:], in1=prods[2][:, cols], op=ADD)
                nc.sync.dma_start(out=out[:, a + cols.start : a + cols.stop], in_=result[:])
